import numpy as np
import ml_dtypes


def mxq(x, axis, fmt="e4m3"):
    dtype, down = {"e4m3": (ml_dtypes.float8_e4m3fn, 7), "e5m2": (ml_dtypes.float8_e5m2, 14)}[fmt]
    v = np.moveaxis(np.asarray(x, np.float32).astype(ml_dtypes.bfloat16).astype(np.float64), axis, -1)
    blocks = v.reshape(v.shape[:-1] + (-1, 32))
    amax = np.abs(blocks).max(-1, keepdims=True)
    byte = np.maximum(np.where(amax > 0, np.frexp(amax)[1] - 1 + 127, 0) - down, 1)
    scale = np.exp2(byte - 127.0)
    codes = (blocks / scale).astype(np.float32).astype(dtype).astype(np.float64)
    return np.moveaxis((codes * scale).reshape(v.shape), -1, axis)


WIDE = False


def mx_kscale(k):
    if not WIDE:
        return np.ones(k)
    levels = np.array([10, -10, 5, -5, 0])
    if k % 512:
        return np.exp2(np.random.permutation(np.resize(levels, k // 32))).repeat(32)
    a = np.empty((k // 512, 16))
    for p in range(k // 512):
        a[p, :8] = np.random.permutation(np.resize(levels, 8))
        for g in range(8):
            far = levels[np.abs(levels - a[p, g]) >= 10]
            a[p, g + 8] = far[np.random.randint(len(far))]
    return np.exp2(a.ravel()).repeat(32)


def f64(x):
    return np.asarray(x).astype(np.float64)


def striped(idx):
    return np.tile(idx.reshape(-1, 16).T, (8, 1)).astype(np.uint16)


def unstriped(offs):
    return offs[:16].T.reshape(-1).astype(np.int64)


def striped8(idx):
    return np.concatenate([x.reshape(-1, 16).T for x in idx]).astype(np.uint16)


def runs(offs, k):
    lists = np.stack([offs[16 * r : 16 * r + 16].T.reshape(-1) for r in range(8)]).astype(np.int64)
    return lists[np.arange(k) % 512 // 64]


def pack_weight(w):
    k, n = w.shape
    w = f64(np.asarray(w, np.float32).astype(ml_dtypes.bfloat16)).reshape(k // 32, 32, n)
    amax = np.abs(w).max(1)
    byte = np.clip(np.where(amax > 0, np.frexp(amax)[1] - 1 + 127 - 7, 1), 1, 254)
    scaled = (w * np.exp2(127.0 - byte)[:, None, :]).reshape(k, n).astype(np.float32)
    words = np.ascontiguousarray(scaled.reshape(k // 512, 128, 4, n).transpose(0, 1, 3, 2)).astype(ml_dtypes.float8_e4m3fn).view(np.uint8)
    return words, np.ascontiguousarray(byte.astype(np.uint8).reshape(k // 512, 16, n))


def unpack_weight(words, scales):
    g, p, n, _ = words.shape
    vals = np.ascontiguousarray(words).view(ml_dtypes.float8_e4m3fn).astype(np.float64) * np.repeat(np.exp2(scales.astype(np.float64) - 127.0), 8, axis=1)[..., None]
    return vals.transpose(0, 1, 3, 2).reshape(g * 512, n)


def sigmoid(v):
    return 1.0 / (1.0 + np.exp(-np.maximum(v, -700.0)))

def planes(y):
    n, m = y.shape
    v = y.astype(np.float32).astype(ml_dtypes.bfloat16).astype(np.float64).reshape(n // 32, 32, m)
    top = np.abs(v).max(1)
    byte = np.clip(np.where(top > 0, np.frexp(top)[1] - 1 + 127 - 7, 1), 1, 254)
    codes = (v * np.exp2(127.0 - byte)[:, None, :]).reshape(n, m).astype(np.float32).astype(ml_dtypes.float8_e4m3fn).view(np.uint8)
    words = codes.reshape(n // 512, 128, 4, m).transpose(0, 1, 3, 2)
    return np.ascontiguousarray(words), np.ascontiguousarray(byte.astype(np.uint8).reshape(n // 512, 16, m))


K, T, S, G, H, C, W = 512, 1024, 256, 2048, 512, 512, 192


def setup_inputs():
    n = np.random.standard_normal
    s = mx_kscale(K)[:, None]
    packed_xT = pack_weight(n((K, T)) * s)
    packed_dT = pack_weight(n((K, G)) / s)
    return {
        "x_words": packed_xT[0],
        "x_scales": packed_xT[1],
        "d_words": packed_dT[0],
        "d_scales": packed_dT[1],
        "sl": np.random.uniform(1.0, 2.0, (H, 1)).astype(np.float32),
        "th": (0.5 * n((H, 1))).astype(np.float32),
        "gs": (np.random.uniform(0.5, 1.5, (K, 1)) / s).astype(np.float32),
        "offs": striped8(np.random.randint(0, T, (8, S))),
        "k1": striped8(np.random.randint(0, G, (8, H))),
        "n1": striped8(np.stack([np.random.permutation(S) for _ in range(8)])),
        "n2": striped8(np.stack([np.random.permutation(S) for _ in range(8)])),
        "cand": striped(np.random.permutation(T)[:C]),
        "n3": striped(np.random.permutation(S)[:W]),
        "n4": striped(np.random.permutation(S)[:W]),
    }


def reference(x_words, x_scales, d_words, d_scales, sl, th, gs, offs, k1, n1, n2, cand, n3, n4):
    x_cand = unpack_weight(x_words, x_scales)[:, unstriped(cand)]
    d_k1 = unpack_weight(d_words, d_scales)[np.arange(K)[:, None], runs(k1, K)]
    xq = unpack_weight(x_words, x_scales)[np.arange(K)[:, None], runs(offs, K)]
    h = 0.0625 * (d_k1.T @ xq)
    st = np.maximum(h, h[np.arange(H)[:, None], runs(n1, H)])
    sg = sigmoid(f64(sl) * (st[np.arange(H)[:, None], runs(n2, H)] - f64(th)))
    z = f64(gs) * (st * sg)
    s = 0.0625 * ((x_cand.T @ mxq(z, 0, "e4m3")))
    old = s[:, unstriped(n3)]
    pa = s[:, unstriped(n4)]
    ra = old - (0.5 * pa)
    out = s.copy()
    out[:, unstriped(n3)] = ra
    return (out,) + planes(out)

@@ -1,0 +1,213 @@
+from contextlib import ExitStack
+
+import concourse.mybir as mybir
+
+F32 = mybir.dt.float32
+BF16 = mybir.dt.bfloat16
+I32 = mybir.dt.int32
+U32 = mybir.dt.uint32
+U16 = mybir.dt.uint16
+U8 = mybir.dt.uint8
+FP8X4 = mybir.dt.float8_e4m3fn_x4
+ALU = mybir.AluOpType
+ACT = mybir.ActivationFunctionType
+
+P = 128
+PACK = 4
+T, S, G, H, C, W = 1024, 256, 2048, 512, 512, 192
+HALF = S // 2
+QUARTER = S // 4
+SIXTEENTH = 0.0625
+FLOPS = 2 * 512 * H * S + 2 * 512 * C * S
+
+
+def tile_picked_hpqcehhkdif_none_po_kernel(
+    tc, x_words, x_scales, d_words, d_scales, sl, th, gs, offs, k1, n1, n2, cand, n3, n4, out_0, out_1, out_2
+):
+    nc = tc.nc
+    with ExitStack() as ctx:
+        keep = ctx.enter_context(tc.tile_pool(name="keep", bufs=1))
+        psum = ctx.enter_context(tc.psum_pool(name="psum", bufs=1))
+
+        def sb(name, shape, dtype, tag=None):
+            return keep.tile(shape, dtype, name=name, tag=tag or name, align_bytes=64)
+
+        def load_list(name, src):
+            tile = sb(name, [P, src.shape[1]], U16)
+            nc.sync.dma_start(tile[:], src)
+            return tile
+
+        def load_byte_table(name, src):
+            columns = src.shape[2]
+            tile = sb(name, [P, columns], U8)
+            rows = src[0].bitcast(I32).unsqueeze(1).to_broadcast([16, 8, columns // 4])
+            nc.scalar.dma_start(tile[:].bitcast(I32), rows)
+            return tile
+
+        def load_word_table(name, src):
+            tile = sb(name, [P, src.shape[2]], U32)
+            nc.sync.dma_start(tile[:].bitcast(I32), src[0].rearrange("p n t -> p (n t)").bitcast(I32))
+            return tile
+
+        def move_scale_rows(dst, src, queues):
+            for q in range(4):
+                queues[q % len(queues)].dma_start(
+                    dst[:].bitcast(I32)[32 * q : 32 * q + 4, :], src[:].bitcast(I32)[32 * q : 32 * q + 32 : 8, :]
+                )
+
+        offs_l = load_list("offs_l", offs)
+        x_byte_table = load_byte_table("x_byte_table", x_scales)
+        k1_l = load_list("k1_l", k1)
+        d_byte_table = load_byte_table("d_byte_table", d_scales)
+        cand_l = load_list("cand_l", cand)
+        n1_l = load_list("n1_l", n1)
+        n2_l = load_list("n2_l", n2)
+        d_word_table = load_word_table("d_word_table", d_words)
+        x_word_table = load_word_table("x_word_table", x_words)
+        n3_l = load_list("n3_l", n3)
+        n4_l = load_list("n4_l", n4)
+        per_row = {}
+        for name, src in (("sl", sl), ("th", th), ("gs", gs)):
+            per_row[name] = sb(name + "_rows", [P, PACK], F32)
+            nc.gpsimd.dma_start(per_row[name][:], src.rearrange("(p t) o -> p (t o)", t=PACK))
+
+        moved_bytes = sb("moved_bytes", [P, H + S], U8)
+        cand_bytes = sb("cand_bytes", [P, C], U8)
+        nc.vector.memset(moved_bytes[:].bitcast(U32), 0)
+        nc.vector.memset(cand_bytes[:].bitcast(U32), 0)
+
+        picked_bytes = sb("picked_bytes", [P, H + S], U8)
+        nc.vector.tensor_copy(picked_bytes[:, H : H + S], x_byte_table[:].indirect(offs_l[:]))
+        nc.vector.tensor_copy(picked_bytes[:, 0:H], d_byte_table[:].indirect(k1_l[:]))
+        move_scale_rows(moved_bytes, picked_bytes, (nc.scalar, nc.sync))
+        cand_picked = sb("cand_picked", [P, C], U8)
+        nc.vector.tensor_copy(
+            cand_picked[:].rearrange("p (t m) -> p m t", t=PACK), x_byte_table[:].indirect(cand_l[:])
+        )
+        move_scale_rows(cand_bytes, cand_picked, (nc.sync,))
+
+        picked_d = sb("picked_d", [P, H], U32)
+        nc.vector.tensor_copy(picked_d[:], d_word_table[:].indirect(k1_l[:]))
+        xq_words = sb("xq_words", [P, S], U32)
+        nc.vector.tensor_copy(xq_words[:], x_word_table[:].indirect(offs_l[:]))
+        dk_words = sb("dk_words", [P, H], U32, tag="stationary_words")
+        nc.vector.tensor_copy(
+            dk_words[:].rearrange("p (t m) -> p m t", t=PACK), picked_d[:].rearrange("p (m t) -> p m t", t=PACK)
+        )
+        dk_bytes = [sb("dk_bytes%d" % t, [P, P], U8) for t in range(PACK)]
+        for t in range(PACK):
+            nc.vector.tensor_copy(dk_bytes[t][:], moved_bytes[:, t:H:PACK])
+
+        product = sb("product", [P, PACK], F32)
+        nc.gpsimd.tensor_tensor(product[:], per_row["sl"][:], per_row["th"][:], ALU.mult)
+        bias = sb("bias", [P, PACK], F32)
+        nc.gpsimd.tensor_scalar(bias[:], product[:], -1.0, 0.0, ALU.mult, ALU.add)
+
+        h_ps, h_sb, near, st = [], [], [], []
+        for t in range(PACK):
+            h_ps.append(psum.tile([P, S], F32, name="h_ps%d" % t))
+            nc.tensor.matmul_mx(
+                out=h_ps[t][:],
+                lhsT=dk_words[:, P * t : P * (t + 1)].bitcast(FP8X4),
+                lhsT_scale=dk_bytes[t][:],
+                rhs=xq_words[:].bitcast(FP8X4),
+                rhs_scale=moved_bytes[:, H : H + S],
+                start=True,
+                stop=True,
+            )
+            h_sb.append(sb("h_sb%d" % t, [P, 2 * S], F32))
+            if t == 0:
+                nc.scalar.activation(out=h_sb[t][:, 0:S], in_=h_ps[t][:], func=ACT.Copy, scale=SIXTEENTH)
+            else:
+                nc.vector.tensor_scalar(h_sb[t][:, 0:S], h_ps[t][:], SIXTEENTH, None, ALU.mult)
+        for t in range(PACK):
+            near.append(sb("near%d" % t, [P, S], F32))
+            nc.scalar.activation(out=near[t][:], in_=h_sb[t][:].indirect(n1_l[:]), func=ACT.Copy)
+
+        cand_words = sb("cand_words", [P, C], U32, tag="stationary_words")
+        nc.vector.tensor_copy(cand_words[:].rearrange("p (t m) -> p m t", t=PACK), x_word_table[:].indirect(cand_l[:]))
+
+        weighted = sb("weighted", [P, PACK, S], F32)
+        for t in range(PACK):
+            st.append(sb("st%d" % t, [P, S], F32))
+            nc.vector.scalar_tensor_tensor(st[t][:], h_ps[t][:], SIXTEENTH, near[t][:], ALU.mult, ALU.max)
+        for t in range(PACK):
+            nc.vector.tensor_scalar(weighted[:, t, :], st[t][:], per_row["gs"][:, t : t + 1], None, ALU.mult)
+
+        s_ps = [psum.tile([P, S], F32, name="s_ps%d" % t) for t in range(PACK)]
+        s_sb = [sb("s%d" % t, [P, S], F32) for t in range(PACK)]
+        for half, widths in ((0, (HALF,)), (1, (HALF,))):
+            h0 = half * HALF
+            gates = sb("gates%d" % half, [P, PACK * HALF], F32, tag="near%d" % (PACK - 1) if half else None)
+            z_words = sb("z_words%d" % half, [P, HALF], U32)
+            z_bytes = sb("z_bytes%d" % half, [P, HALF], U8)
+            for piece, width in enumerate(widths):
+                p0 = piece * width
+                c0 = h0 + p0
+                gate = gates[:, PACK * p0 : PACK * (p0 + width)].rearrange("p (t c) -> p t c", t=PACK)
+                for t in range(PACK):
+                    nc.scalar.activation(
+                        out=gate[:, t, :],
+                        in_=st[t][:].indirect(n2_l[:, c0 // 16 : (c0 + width) // 16]),
+                        func=ACT.Sigmoid,
+                        scale=per_row["sl"][:, t : t + 1],
+                        bias=bias[:, t : t + 1],
+                    )
+                z = sb("z%d" % c0, [P, width * PACK], BF16)
+                nc.vector.tensor_tensor(
+                    z[:].rearrange("p (c i t) -> p c t i", i=4, t=PACK),
+                    weighted[:, :, c0 : c0 + width].rearrange("p t (c i) -> p c t i", i=4),
+                    gate.rearrange("p t (c i) -> p c t i", i=4),
+                    ALU.mult,
+                )
+                nc.vector.quantize_mx(
+                    out=z_words[:, p0 : p0 + width].bitcast(FP8X4), scales=z_bytes[:, p0 : p0 + width], in_=z[:]
+                )
+            for t in range(PACK):
+                nc.tensor.matmul_mx(
+                    out=s_ps[t][:, h0 : h0 + HALF],
+                    lhsT=cand_words[:, P * t : P * (t + 1)].bitcast(FP8X4),
+                    lhsT_scale=cand_bytes[:, P * t : P * (t + 1)],
+                    rhs=z_words[:].bitcast(FP8X4),
+                    rhs_scale=z_bytes[:],
+                    start=True,
+                    stop=True,
+                )
+            nc.vector.tensor_scalar(
+                s_sb[0][:, h0 : h0 + HALF], s_ps[0][:, h0 : h0 + HALF], SIXTEENTH, None, ALU.mult
+            )
+
+        rounded = [sb("rounded%d" % half, [P, HALF, PACK], BF16) for half in range(2)]
+        out_rows = out_0.rearrange("(p t) j -> p t j", t=PACK)
+        for t in range(PACK):
+            s = s_sb[t]
+            if t > 0:
+                nc.vector.tensor_scalar(s[:], s_ps[t][:], SIXTEENTH, None, ALU.mult)
+            result = sb("result%d" % t, [P, S], F32)
+            nc.vector.tensor_copy(result[:], s[:])
+            old = sb("old%d" % t, [P, W], F32)
+            pa = sb("pa%d" % t, [P, W], F32)
+            nc.scalar.activation(out=old[:], in_=s[:].indirect(n3_l[:]), func=ACT.Copy)
+            nc.scalar.activation(out=pa[:], in_=s[:].indirect(n4_l[:]), func=ACT.Copy)
+            ra = sb("ra%d" % t, [P, W], F32)
+            nc.vector.scalar_tensor_tensor(ra[:], pa[:], -0.5, old[:], ALU.mult, ALU.add)
+            nc.scalar.activation(out=result[:].indirect(n3_l[:]), in_=ra[:], func=ACT.Copy)
+            nc.sync.dma_start(out_rows[:, t, :], result[:])
+            for half in range(2):
+                nc.vector.tensor_copy(rounded[half][:, :, t], result[:, half * HALF : (half + 1) * HALF])
+
+        out_words = sb("out_words", [P, S], U32)
+        out_bytes = sb("out_bytes", [P, S], U8)
+        for half in range(2):
+            columns = slice(half * HALF, (half + 1) * HALF)
+            nc.vector.quantize_mx(
+                out=out_words[:, columns].bitcast(FP8X4),
+                scales=out_bytes[:, columns],
+                in_=rounded[half][:].rearrange("p j t -> p (j t)"),
+            )
+        nc.sync.dma_start(out_1[0].rearrange("p n t -> p (n t)").bitcast(I32), out_words[:].bitcast(I32))
+        for q in range(4):
+            queue = nc.scalar if q % 2 == 0 else nc.sync
+            queue.dma_start(
+                out_2[0].bitcast(I32)[4 * q : 4 * q + 4, :], out_bytes[:].bitcast(I32)[32 * q : 32 * q + 4, :]
+            )

@@ -76,6 +76,11 @@ def tile_picked_hpqcehhkdif_none_po_kernel(
         nc.vector.memset(moved_bytes[:].bitcast(U32), 0)
         nc.vector.memset(cand_bytes[:].bitcast(U32), 0)
 
+        warm_in = sb("warm_in", [P, 1], F32)
+        warm_out = sb("warm_out", [P, 1], F32)
+        nc.vector.memset(warm_in[:], 0.0)
+        nc.scalar.activation(out=warm_out[:], in_=warm_in[:], func=ACT.Sigmoid)
+
         picked_bytes = sb("picked_bytes", [P, H + S], U8)
         nc.vector.tensor_copy(picked_bytes[:, H : H + S], x_byte_table[:].indirect(offs_l[:]))
         nc.vector.tensor_copy(picked_bytes[:, 0:H], d_byte_table[:].indirect(k1_l[:]))

@@ -14,11 +14,19 @@ ACT = mybir.ActivationFunctionType
 
 P = 128
 PACK = 4
-T, S, G, H, C, W = 1024, 256, 2048, 512, 512, 192
+K = 512
+S = 256
+H = 512
+C = 512
+W = 192
+LIST_ROWS = 16
+SCALE_ROWS = K // 32
+QUADRANT = 32
 HALF = S // 2
 QUARTER = S // 4
 SIXTEENTH = 0.0625
-FLOPS = 2 * 512 * H * S + 2 * 512 * C * S
+Z_PIECES = ((HALF,), (QUARTER, QUARTER))
+FLOPS = 2 * K * H * S + 2 * K * C * S
 
 
 def tile_picked_hpqcehhkdif_none_po_kernel(
@@ -40,7 +48,7 @@ def tile_picked_hpqcehhkdif_none_po_kernel(
         def load_byte_table(name, src):
             columns = src.shape[2]
             tile = sb(name, [P, columns], U8)
-            rows = src[0].bitcast(I32).unsqueeze(1).to_broadcast([16, 8, columns // 4])
+            rows = src[0].bitcast(I32).unsqueeze(1).to_broadcast([SCALE_ROWS, P // SCALE_ROWS, columns // 4])
             nc.scalar.dma_start(tile[:].bitcast(I32), rows)
             return tile
 
@@ -50,9 +58,10 @@ def tile_picked_hpqcehhkdif_none_po_kernel(
             return tile
 
         def move_scale_rows(dst, src, queues):
-            for q in range(4):
-                queues[q % len(queues)].dma_start(
-                    dst[:].bitcast(I32)[32 * q : 32 * q + 4, :], src[:].bitcast(I32)[32 * q : 32 * q + 32 : 8, :]
+            for quadrant in range(P // QUADRANT):
+                base = QUADRANT * quadrant
+                queues[quadrant % len(queues)].dma_start(
+                    dst[:].bitcast(I32)[base : base + 4, :], src[:].bitcast(I32)[base : base + QUADRANT : 8, :]
                 )
 
         offs_l = load_list("offs_l", offs)
@@ -81,7 +90,7 @@ def tile_picked_hpqcehhkdif_none_po_kernel(
         nc.vector.memset(warm_in[:], 0.0)
         nc.scalar.activation(out=warm_out[:], in_=warm_in[:], func=ACT.Sigmoid)
 
-        picked_bytes = sb("picked_bytes", [P, H + S], U8)
+        picked_bytes = sb("picked_bytes", [P, H + S], U8, tag="stationary")
         nc.vector.tensor_copy(picked_bytes[:, H : H + S], x_byte_table[:].indirect(offs_l[:]))
         nc.vector.tensor_copy(picked_bytes[:, 0:H], d_byte_table[:].indirect(k1_l[:]))
         move_scale_rows(moved_bytes, picked_bytes, (nc.scalar, nc.sync))
@@ -95,18 +104,16 @@ def tile_picked_hpqcehhkdif_none_po_kernel(
         nc.vector.tensor_copy(picked_d[:], d_word_table[:].indirect(k1_l[:]))
         xq_words = sb("xq_words", [P, S], U32)
         nc.vector.tensor_copy(xq_words[:], x_word_table[:].indirect(offs_l[:]))
-        dk_words = sb("dk_words", [P, H], U32, tag="stationary_words")
-        nc.vector.tensor_copy(
-            dk_words[:].rearrange("p (t m) -> p m t", t=PACK), picked_d[:].rearrange("p (m t) -> p m t", t=PACK)
-        )
+        dk_words = sb("dk_words", [P, H], U32, tag="stationary")
         dk_bytes = [sb("dk_bytes%d" % t, [P, P], U8) for t in range(PACK)]
         for t in range(PACK):
+            nc.vector.tensor_copy(dk_words[:, P * t : P * (t + 1)], picked_d[:, t:H:PACK])
             nc.vector.tensor_copy(dk_bytes[t][:], moved_bytes[:, t:H:PACK])
 
-        product = sb("product", [P, PACK], F32)
-        nc.gpsimd.tensor_tensor(product[:], per_row["sl"][:], per_row["th"][:], ALU.mult)
+        sl_th = sb("sl_th", [P, PACK], F32)
+        nc.gpsimd.tensor_tensor(sl_th[:], per_row["sl"][:], per_row["th"][:], ALU.mult)
         bias = sb("bias", [P, PACK], F32)
-        nc.gpsimd.tensor_scalar(bias[:], product[:], -1.0, 0.0, ALU.mult, ALU.add)
+        nc.gpsimd.tensor_scalar(bias[:], sl_th[:], -1.0, 0.0, ALU.mult, ALU.add)
 
         h_ps, h_sb, near, st = [], [], [], []
         for t in range(PACK):
@@ -129,7 +136,7 @@ def tile_picked_hpqcehhkdif_none_po_kernel(
             near.append(sb("near%d" % t, [P, S], F32))
             nc.scalar.activation(out=near[t][:], in_=h_sb[t][:].indirect(n1_l[:]), func=ACT.Copy)
 
-        cand_words = sb("cand_words", [P, C], U32, tag="stationary_words")
+        cand_words = sb("cand_words", [P, C], U32, tag="stationary")
         nc.vector.tensor_copy(cand_words[:].rearrange("p (t m) -> p m t", t=PACK), x_word_table[:].indirect(cand_l[:]))
 
         weighted = sb("weighted", [P, PACK, S], F32)
@@ -139,9 +146,20 @@ def tile_picked_hpqcehhkdif_none_po_kernel(
         for t in range(PACK):
             nc.vector.tensor_scalar(weighted[:, t, :], st[t][:], per_row["gs"][:, t : t + 1], None, ALU.mult)
 
-        s_ps = [psum.tile([P, S], F32, name="s_ps%d" % t) for t in range(PACK)]
+        def score(acc, t, words, scales):
+            nc.tensor.matmul_mx(
+                out=acc,
+                lhsT=cand_words[:, P * t : P * (t + 1)].bitcast(FP8X4),
+                lhsT_scale=cand_bytes[:, P * t : P * (t + 1)],
+                rhs=words.bitcast(FP8X4),
+                rhs_scale=scales,
+                start=True,
+                stop=True,
+            )
+
+        s_ps = {t: psum.tile([P, S], F32, name="s_ps%d" % t) for t in range(1, PACK)}
         s_sb = [sb("s%d" % t, [P, S], F32) for t in range(PACK)]
-        for half, widths in ((0, (HALF,)), (1, (HALF,))):
+        for half, widths in enumerate(Z_PIECES):
             h0 = half * HALF
             gates = sb("gates%d" % half, [P, PACK * HALF], F32, tag="near%d" % (PACK - 1) if half else None)
             z_words = sb("z_words%d" % half, [P, HALF], U32)
@@ -153,7 +171,7 @@ def tile_picked_hpqcehhkdif_none_po_kernel(
                 for t in range(PACK):
                     nc.scalar.activation(
                         out=gate[:, t, :],
-                        in_=st[t][:].indirect(n2_l[:, c0 // 16 : (c0 + width) // 16]),
+                        in_=st[t][:].indirect(n2_l[:, c0 // LIST_ROWS : (c0 + width) // LIST_ROWS]),
                         func=ACT.Sigmoid,
                         scale=per_row["sl"][:, t : t + 1],
                         bias=bias[:, t : t + 1],
@@ -168,19 +186,11 @@ def tile_picked_hpqcehhkdif_none_po_kernel(
                 nc.vector.quantize_mx(
                     out=z_words[:, p0 : p0 + width].bitcast(FP8X4), scales=z_bytes[:, p0 : p0 + width], in_=z[:]
                 )
-            for t in range(PACK):
-                nc.tensor.matmul_mx(
-                    out=s_ps[t][:, h0 : h0 + HALF],
-                    lhsT=cand_words[:, P * t : P * (t + 1)].bitcast(FP8X4),
-                    lhsT_scale=cand_bytes[:, P * t : P * (t + 1)],
-                    rhs=z_words[:].bitcast(FP8X4),
-                    rhs_scale=z_bytes[:],
-                    start=True,
-                    stop=True,
-                )
-            nc.vector.tensor_scalar(
-                s_sb[0][:, h0 : h0 + HALF], s_ps[0][:, h0 : h0 + HALF], SIXTEENTH, None, ALU.mult
-            )
+                first = psum.tile([P, width], F32, name="first%d" % c0, tag="h_ps%d" % (half + piece))
+                score(first[:], 0, z_words[:, p0 : p0 + width], z_bytes[:, p0 : p0 + width])
+                nc.vector.tensor_scalar(s_sb[0][:, c0 : c0 + width], first[:], SIXTEENTH, None, ALU.mult)
+            for t in range(1, PACK):
+                score(s_ps[t][:, h0 : h0 + HALF], t, z_words[:], z_bytes[:])
 
         rounded = [sb("rounded%d" % half, [P, HALF, PACK], BF16) for half in range(2)]
         out_rows = out_0.rearrange("(p t) j -> p t j", t=PACK)
@@ -211,8 +221,9 @@ def tile_picked_hpqcehhkdif_none_po_kernel(
                 in_=rounded[half][:].rearrange("p j t -> p (j t)"),
             )
         nc.sync.dma_start(out_1[0].rearrange("p n t -> p (n t)").bitcast(I32), out_words[:].bitcast(I32))
-        for q in range(4):
-            queue = nc.scalar if q % 2 == 0 else nc.sync
+        for quadrant in range(P // QUADRANT):
+            queue = nc.scalar if quadrant % 2 == 0 else nc.sync
             queue.dma_start(
-                out_2[0].bitcast(I32)[4 * q : 4 * q + 4, :], out_bytes[:].bitcast(I32)[32 * q : 32 * q + 4, :]
+                out_2[0].bitcast(I32)[4 * quadrant : 4 * quadrant + 4, :],
+                out_bytes[:].bitcast(I32)[QUADRANT * quadrant : QUADRANT * quadrant + 4, :],
             )

from contextlib import ExitStack

import concourse.mybir as mybir

F32 = mybir.dt.float32
BF16 = mybir.dt.bfloat16
I32 = mybir.dt.int32
U32 = mybir.dt.uint32
U16 = mybir.dt.uint16
U8 = mybir.dt.uint8
FP8X4 = mybir.dt.float8_e4m3fn_x4
ALU = mybir.AluOpType
ACT = mybir.ActivationFunctionType

P = 128
PACK = 4
K = 512
S = 256
H = 512
C = 512
W = 192
LIST_ROWS = 16
SCALE_ROWS = K // 32
QUADRANT = 32
HALF = S // 2
QUARTER = S // 4
SIXTEENTH = 0.0625
Z_PIECES = ((HALF,), (QUARTER, QUARTER))
FLOPS = 2 * K * H * S + 2 * K * C * S


def tile_picked_hpqcehhkdif_none_po_kernel(
    tc, x_words, x_scales, d_words, d_scales, sl, th, gs, offs, k1, n1, n2, cand, n3, n4, out_0, out_1, out_2
):
    nc = tc.nc
    with ExitStack() as ctx:
        keep = ctx.enter_context(tc.tile_pool(name="keep", bufs=1))
        psum = ctx.enter_context(tc.psum_pool(name="psum", bufs=1))

        def sb(name, shape, dtype, tag=None):
            return keep.tile(shape, dtype, name=name, tag=tag or name, align_bytes=64)

        def load_list(name, src):
            tile = sb(name, [P, src.shape[1]], U16)
            nc.sync.dma_start(tile[:], src)
            return tile

        def load_byte_table(name, src):
            columns = src.shape[2]
            tile = sb(name, [P, columns], U8)
            rows = src[0].bitcast(I32).unsqueeze(1).to_broadcast([SCALE_ROWS, P // SCALE_ROWS, columns // 4])
            nc.scalar.dma_start(tile[:].bitcast(I32), rows)
            return tile

        def load_word_table(name, src):
            tile = sb(name, [P, src.shape[2]], U32)
            nc.sync.dma_start(tile[:].bitcast(I32), src[0].rearrange("p n t -> p (n t)").bitcast(I32))
            return tile

        def move_scale_rows(dst, src, queues):
            for quadrant in range(P // QUADRANT):
                base = QUADRANT * quadrant
                queues[quadrant % len(queues)].dma_start(
                    dst[:].bitcast(I32)[base : base + 4, :], src[:].bitcast(I32)[base : base + QUADRANT : 8, :]
                )

        offs_l = load_list("offs_l", offs)
        x_byte_table = load_byte_table("x_byte_table", x_scales)
        k1_l = load_list("k1_l", k1)
        d_byte_table = load_byte_table("d_byte_table", d_scales)
        cand_l = load_list("cand_l", cand)
        n1_l = load_list("n1_l", n1)
        n2_l = load_list("n2_l", n2)
        d_word_table = load_word_table("d_word_table", d_words)
        x_word_table = load_word_table("x_word_table", x_words)
        n3_l = load_list("n3_l", n3)
        n4_l = load_list("n4_l", n4)
        per_row = {}
        for name, src in (("sl", sl), ("th", th), ("gs", gs)):
            per_row[name] = sb(name + "_rows", [P, PACK], F32)
            nc.gpsimd.dma_start(per_row[name][:], src.rearrange("(p t) o -> p (t o)", t=PACK))

        moved_bytes = sb("moved_bytes", [P, H + S], U8)
        cand_bytes = sb("cand_bytes", [P, C], U8)
        nc.vector.memset(moved_bytes[:].bitcast(U32), 0)
        nc.vector.memset(cand_bytes[:].bitcast(U32), 0)

        warm_in = sb("warm_in", [P, 1], F32)
        warm_out = sb("warm_out", [P, 1], F32)
        nc.vector.memset(warm_in[:], 0.0)
        nc.scalar.activation(out=warm_out[:], in_=warm_in[:], func=ACT.Sigmoid)

        picked_bytes = sb("picked_bytes", [P, H + S], U8, tag="stationary")
        nc.vector.tensor_copy(picked_bytes[:, H : H + S], x_byte_table[:].indirect(offs_l[:]))
        nc.vector.tensor_copy(picked_bytes[:, 0:H], d_byte_table[:].indirect(k1_l[:]))
        move_scale_rows(moved_bytes, picked_bytes, (nc.scalar, nc.sync))
        cand_picked = sb("cand_picked", [P, C], U8)
        nc.vector.tensor_copy(
            cand_picked[:].rearrange("p (t m) -> p m t", t=PACK), x_byte_table[:].indirect(cand_l[:])
        )
        move_scale_rows(cand_bytes, cand_picked, (nc.sync,))

        picked_d = sb("picked_d", [P, H], U32)
        nc.vector.tensor_copy(picked_d[:], d_word_table[:].indirect(k1_l[:]))
        xq_words = sb("xq_words", [P, S], U32)
        nc.vector.tensor_copy(xq_words[:], x_word_table[:].indirect(offs_l[:]))
        dk_words = sb("dk_words", [P, H], U32, tag="stationary")
        dk_bytes = [sb("dk_bytes%d" % t, [P, P], U8) for t in range(PACK)]
        for t in range(PACK):
            nc.vector.tensor_copy(dk_words[:, P * t : P * (t + 1)], picked_d[:, t:H:PACK])
            nc.vector.tensor_copy(dk_bytes[t][:], moved_bytes[:, t:H:PACK])

        sl_th = sb("sl_th", [P, PACK], F32)
        nc.gpsimd.tensor_tensor(sl_th[:], per_row["sl"][:], per_row["th"][:], ALU.mult)
        bias = sb("bias", [P, PACK], F32)
        nc.gpsimd.tensor_scalar(bias[:], sl_th[:], -1.0, 0.0, ALU.mult, ALU.add)

        h_ps, h_sb, near, st = [], [], [], []
        for t in range(PACK):
            h_ps.append(psum.tile([P, S], F32, name="h_ps%d" % t))
            nc.tensor.matmul_mx(
                out=h_ps[t][:],
                lhsT=dk_words[:, P * t : P * (t + 1)].bitcast(FP8X4),
                lhsT_scale=dk_bytes[t][:],
                rhs=xq_words[:].bitcast(FP8X4),
                rhs_scale=moved_bytes[:, H : H + S],
                start=True,
                stop=True,
            )
            h_sb.append(sb("h_sb%d" % t, [P, 2 * S], F32))
            if t == 0:
                nc.scalar.activation(out=h_sb[t][:, 0:S], in_=h_ps[t][:], func=ACT.Copy, scale=SIXTEENTH)
            else:
                nc.vector.tensor_scalar(h_sb[t][:, 0:S], h_ps[t][:], SIXTEENTH, None, ALU.mult)
        for t in range(PACK):
            near.append(sb("near%d" % t, [P, S], F32))
            nc.scalar.activation(out=near[t][:], in_=h_sb[t][:].indirect(n1_l[:]), func=ACT.Copy)

        cand_words = sb("cand_words", [P, C], U32, tag="stationary")
        nc.vector.tensor_copy(cand_words[:].rearrange("p (t m) -> p m t", t=PACK), x_word_table[:].indirect(cand_l[:]))

        weighted = sb("weighted", [P, PACK, S], F32)
        for t in range(PACK):
            st.append(sb("st%d" % t, [P, S], F32))
            nc.vector.scalar_tensor_tensor(st[t][:], h_ps[t][:], SIXTEENTH, near[t][:], ALU.mult, ALU.max)
        for t in range(PACK):
            nc.vector.tensor_scalar(weighted[:, t, :], st[t][:], per_row["gs"][:, t : t + 1], None, ALU.mult)

        def score(acc, t, words, scales):
            nc.tensor.matmul_mx(
                out=acc,
                lhsT=cand_words[:, P * t : P * (t + 1)].bitcast(FP8X4),
                lhsT_scale=cand_bytes[:, P * t : P * (t + 1)],
                rhs=words.bitcast(FP8X4),
                rhs_scale=scales,
                start=True,
                stop=True,
            )

        s_ps = {t: psum.tile([P, S], F32, name="s_ps%d" % t) for t in range(1, PACK)}
        s_sb = [sb("s%d" % t, [P, S], F32) for t in range(PACK)]
        for half, widths in enumerate(Z_PIECES):
            h0 = half * HALF
            gates = sb("gates%d" % half, [P, PACK * HALF], F32, tag="near%d" % (PACK - 1) if half else None)
            z_words = sb("z_words%d" % half, [P, HALF], U32)
            z_bytes = sb("z_bytes%d" % half, [P, HALF], U8)
            for piece, width in enumerate(widths):
                p0 = piece * width
                c0 = h0 + p0
                gate = gates[:, PACK * p0 : PACK * (p0 + width)].rearrange("p (t c) -> p t c", t=PACK)
                for t in range(PACK):
                    nc.scalar.activation(
                        out=gate[:, t, :],
                        in_=st[t][:].indirect(n2_l[:, c0 // LIST_ROWS : (c0 + width) // LIST_ROWS]),
                        func=ACT.Sigmoid,
                        scale=per_row["sl"][:, t : t + 1],
                        bias=bias[:, t : t + 1],
                    )
                z = sb("z%d" % c0, [P, width * PACK], BF16)
                nc.vector.tensor_tensor(
                    z[:].rearrange("p (c i t) -> p c t i", i=4, t=PACK),
                    weighted[:, :, c0 : c0 + width].rearrange("p t (c i) -> p c t i", i=4),
                    gate.rearrange("p t (c i) -> p c t i", i=4),
                    ALU.mult,
                )
                nc.vector.quantize_mx(
                    out=z_words[:, p0 : p0 + width].bitcast(FP8X4), scales=z_bytes[:, p0 : p0 + width], in_=z[:]
                )
                first = psum.tile([P, width], F32, name="first%d" % c0, tag="h_ps%d" % (half + piece))
                score(first[:], 0, z_words[:, p0 : p0 + width], z_bytes[:, p0 : p0 + width])
                nc.vector.tensor_scalar(s_sb[0][:, c0 : c0 + width], first[:], SIXTEENTH, None, ALU.mult)
            for t in range(1, PACK):
                score(s_ps[t][:, h0 : h0 + HALF], t, z_words[:], z_bytes[:])

        rounded = [sb("rounded%d" % half, [P, HALF, PACK], BF16) for half in range(2)]
        out_rows = out_0.rearrange("(p t) j -> p t j", t=PACK)
        for t in range(PACK):
            s = s_sb[t]
            if t > 0:
                nc.vector.tensor_scalar(s[:], s_ps[t][:], SIXTEENTH, None, ALU.mult)
            result = sb("result%d" % t, [P, S], F32)
            nc.vector.tensor_copy(result[:], s[:])
            old = sb("old%d" % t, [P, W], F32)
            pa = sb("pa%d" % t, [P, W], F32)
            nc.scalar.activation(out=old[:], in_=s[:].indirect(n3_l[:]), func=ACT.Copy)
            nc.scalar.activation(out=pa[:], in_=s[:].indirect(n4_l[:]), func=ACT.Copy)
            ra = sb("ra%d" % t, [P, W], F32)
            nc.vector.scalar_tensor_tensor(ra[:], pa[:], -0.5, old[:], ALU.mult, ALU.add)
            nc.scalar.activation(out=result[:].indirect(n3_l[:]), in_=ra[:], func=ACT.Copy)
            nc.sync.dma_start(out_rows[:, t, :], result[:])
            for half in range(2):
                nc.vector.tensor_copy(rounded[half][:, :, t], result[:, half * HALF : (half + 1) * HALF])

        out_words = sb("out_words", [P, S], U32)
        out_bytes = sb("out_bytes", [P, S], U8)
        for half in range(2):
            columns = slice(half * HALF, (half + 1) * HALF)
            nc.vector.quantize_mx(
                out=out_words[:, columns].bitcast(FP8X4),
                scales=out_bytes[:, columns],
                in_=rounded[half][:].rearrange("p j t -> p (j t)"),
            )
        nc.sync.dma_start(out_1[0].rearrange("p n t -> p (n t)").bitcast(I32), out_words[:].bitcast(I32))
        for quadrant in range(P // QUADRANT):
            queue = nc.scalar if quadrant % 2 == 0 else nc.sync
            queue.dma_start(
                out_2[0].bitcast(I32)[4 * quadrant : 4 * quadrant + 4, :],
                out_bytes[:].bitcast(I32)[QUADRANT * quadrant : QUADRANT * quadrant + 4, :],
            )
